import numpy as np
import ml_dtypes


def mxq(x, axis, fmt="e4m3"):
    dtype, down = {"e4m3": (ml_dtypes.float8_e4m3fn, 7), "e5m2": (ml_dtypes.float8_e5m2, 14)}[fmt]
    v = np.moveaxis(np.asarray(x, np.float32).astype(ml_dtypes.bfloat16).astype(np.float64), axis, -1)
    blocks = v.reshape(v.shape[:-1] + (-1, 32))
    amax = np.abs(blocks).max(-1, keepdims=True)
    byte = np.maximum(np.where(amax > 0, np.frexp(amax)[1] - 1 + 127, 0) - down, 1)
    scale = np.exp2(byte - 127.0)
    codes = (blocks / scale).astype(np.float32).astype(dtype).astype(np.float64)
    return np.moveaxis((codes * scale).reshape(v.shape), -1, axis)


WIDE = False


def mx_kscale(k):
    if not WIDE:
        return np.ones(k)
    levels = np.array([10, -10, 5, -5, 0])
    if k % 512:
        return np.exp2(np.random.permutation(np.resize(levels, k // 32))).repeat(32)
    a = np.empty((k // 512, 16))
    for p in range(k // 512):
        a[p, :8] = np.random.permutation(np.resize(levels, 8))
        for g in range(8):
            far = levels[np.abs(levels - a[p, g]) >= 10]
            a[p, g + 8] = far[np.random.randint(len(far))]
    return np.exp2(a.ravel()).repeat(32)


def f64(x):
    return np.asarray(x).astype(np.float64)


def striped(idx):
    return np.tile(idx.reshape(-1, 16).T, (8, 1)).astype(np.uint16)


def unstriped(offs):
    return offs[:16].T.reshape(-1).astype(np.int64)


E2M1 = np.array([0.0, 0.5, 1.0, 1.5, 2.0, 3.0, 4.0, 6.0, -0.0, -0.5, -1.0, -1.5, -2.0, -3.0, -4.0, -6.0])


def pack_fp4(w):
    k, n = w.shape
    w = f64(np.asarray(w, np.float32).astype(ml_dtypes.bfloat16)).reshape(k // 32, 32, n)
    amax = np.abs(w).max(1)
    mant, ex = np.frexp(amax / 6.0)
    byte = np.clip(np.where(amax > 0, np.where(mant > 0.5, ex, ex - 1) + 127, 1), 1, 254)
    scaled = (w * np.exp2(127.0 - byte)[:, None, :]).reshape(k, n).astype(np.float32)
    c = np.ascontiguousarray(scaled.reshape(k // 512, 128, 4, n).transpose(0, 1, 3, 2)).astype(ml_dtypes.float4_e2m1fn).view(np.uint8) & 0xF
    words = (c[..., 0::2] | (c[..., 1::2] << 4)).reshape(k // 512, 128, 2 * n)
    return np.ascontiguousarray(words), np.ascontiguousarray(byte.astype(np.uint8).reshape(k // 512, 16, n))


def unpack_fp4(words, scales):
    g, _, n = scales.shape
    words = np.ascontiguousarray(words).reshape(g, 128, n, 2)
    nib = np.empty((g, 128, n, 4), np.uint8)
    nib[..., 0::2] = words & 0xF
    nib[..., 1::2] = words >> 4
    vals = E2M1[nib] * np.repeat(np.exp2(scales.astype(np.float64) - 127.0), 8, axis=1)[..., None]
    return vals.transpose(0, 1, 3, 2).reshape(g * 512, n)


K, T, S, V, N = 1024, 2048, 512, 256, 256


def setup_inputs():
    n = np.random.standard_normal
    s = mx_kscale(K)[:, None]
    packed_w1 = pack_fp4(n((K, N)) / np.sqrt(K) / s)
    return {
        "xT": (n((K, T)) * s).astype(np.float32),
        "w1_words": packed_w1[0],
        "w1_scales": packed_w1[1],
        "offs": striped(np.random.permutation(T)[:S]),
        "win": striped(np.random.permutation(S)[:V]),
        "lose": striped(np.random.permutation(S)[:V]),
    }


def reference(xT, w1_words, w1_scales, offs, win, lose):
    xq = mxq(f64(xT)[:, unstriped(offs)], 0, "e4m3")
    y = unpack_fp4(w1_words, w1_scales).T @ xq
    return np.tanh(y[:, unstriped(win)] - y[:, unstriped(lose)])

@@ -1,0 +1,107 @@
+from contextlib import ExitStack
+
+import concourse.mybir as mybir
+
+K, T, S, V, N = 1024, 2048, 512, 256, 256
+FLOPS = 2 * K * N * S
+
+F32 = mybir.dt.float32
+BF16 = mybir.dt.bfloat16
+I32 = mybir.dt.int32
+U32 = mybir.dt.uint32
+U16 = mybir.dt.uint16
+U8 = mybir.dt.uint8
+FP8X4 = mybir.dt.float8_e4m3fn_x4
+FP4X4 = mybir.dt.float4_e2m1fn_x4
+TANH = mybir.ActivationFunctionType.Tanh
+SUBTRACT = mybir.AluOpType.subtract
+
+P = 128
+PACK = 4
+K_PASS = P * PACK
+PASSES = K // K_PASS
+M_TILES = N // P
+HALF = S // 2
+SLICE = 128
+SLICES = S // SLICE
+PER_COLUMN = 16
+
+
+def tile_picked_ranknet_tanh_e_kernel(tc, xT, w1_words, w1_scales, offs, win, lose, out):
+    nc = tc.nc
+    with ExitStack() as ctx:
+        keep = ctx.enter_context(tc.tile_pool(name="keep", bufs=1))
+        psum = ctx.enter_context(tc.psum_pool(name="psum", bufs=1))
+
+        offs_sb = keep.tile([P, S // PER_COLUMN], U16, name="offs_sb")
+        win_sb = keep.tile([P, V // PER_COLUMN], U16, name="win_sb")
+        lose_sb = keep.tile([P, V // PER_COLUMN], U16, name="lose_sb")
+        w_codes = keep.tile([P, PASSES, 2 * N], U8, name="w_codes", align_bytes=64)
+        w_scales = keep.tile([P, PASSES, N], U8, name="w_scales", align_bytes=64)
+        warm = keep.tile([P, 8], F32, name="warm")
+        warm2 = keep.tile([P, 8], F32, name="warm2")
+
+        rows = xT.rearrange("(g p t) c -> g t p c", p=P, t=PACK)
+        planes = [[keep.tile([P, T], F32, name="plane_%d_%d" % (g, t)) for t in range(PACK)] for g in range(PASSES)]
+        for g in range(PASSES):
+            for t in range(PACK):
+                nc.sync.dma_start(out=planes[g][t][:], in_=rows[g, t])
+                if g == 0 and t == 0:
+                    nc.sync.dma_start(offs_sb[:], offs)
+        nc.sync.dma_start(out=w_codes[:].bitcast(I32), in_=w1_words.rearrange("g p b -> p g b").bitcast(I32))
+        nc.sync.dma_start(lose_sb[:], lose)
+        nc.sync.dma_start(win_sb[:], win)
+
+        nc.vector.memset(warm[:], 0.0)
+        nc.scalar.activation(warm2[:], warm[:], TANH)
+
+        nc.gpsimd.memset(w_scales[:].rearrange("p g c -> p (g c)").bitcast(I32), 0)
+        for q in range(4):
+            nc.gpsimd.dma_start(
+                out=w_scales[32 * q : 32 * q + 4, :, :].bitcast(I32),
+                in_=w1_scales[:, 4 * q : 4 * q + 4, :].rearrange("g r c -> r g c").bitcast(I32),
+            )
+
+        banks = [[psum.tile([P, SLICE], F32, name="bank_%d_%d" % (m, s)) for s in range(SLICES)] for m in range(M_TILES)]
+        scores = [keep.tile([P, S], F32, name="scores_%d" % m) for m in range(M_TILES)]
+
+        for g in range(PASSES):
+            grouped = [keep.tile([P, HALF, PACK], BF16, name="grouped_%d_%d" % (g, h), align_bytes=64) for h in range(2)]
+            for t in range(PACK):
+                for h in range(2):
+                    cols = slice(h * HALF // PER_COLUMN, (h + 1) * HALF // PER_COLUMN)
+                    nc.vector.tensor_copy(grouped[h][:, :, t], planes[g][t][:].indirect(offs_sb[:, cols]))
+            x_codes = [keep.tile([P, SLICE], U32, name="x_codes_%d_%d" % (g, s), align_bytes=64) for s in range(SLICES)]
+            x_scales = [keep.tile([P, SLICE], U8, name="x_scales_%d_%d" % (g, s), align_bytes=64) for s in range(SLICES)]
+            for s in range(SLICES):
+                h, part = divmod(s, 2)
+                nc.vector.quantize_mx(
+                    out=x_codes[s][:].bitcast(FP8X4),
+                    scales=x_scales[s][:],
+                    in_=grouped[h][:].rearrange("p c t -> p (c t)")[:, part * SLICE * PACK : (part + 1) * SLICE * PACK],
+                )
+            for m in range(M_TILES):
+                for s in range(SLICES):
+                    nc.tensor.matmul_mx(
+                        out=banks[m][s][:],
+                        lhsT=w_codes[:, g, 2 * P * m : 2 * P * (m + 1)].bitcast(FP4X4),
+                        lhsT_scale=w_scales[:, g, P * m : P * (m + 1)],
+                        rhs=x_codes[s][:].bitcast(FP8X4),
+                        rhs_scale=x_scales[s][:],
+                        start=(g == 0),
+                        stop=(g == PASSES - 1),
+                    )
+
+        for m in range(M_TILES):
+            for s in range(SLICES):
+                nc.scalar.copy(scores[m][:, s * SLICE : (s + 1) * SLICE], banks[m][s][:])
+
+        losers = [keep.tile([P, V], F32, name="losers_%d" % m) for m in range(M_TILES)]
+        for m in range(M_TILES):
+            nc.vector.tensor_copy(losers[m][:], scores[m][:].indirect(lose_sb[:]))
+        for m in range(M_TILES):
+            margin = keep.tile([P, V], F32, name="margin_%d" % m)
+            result = keep.tile([P, V], F32, name="result_%d" % m)
+            nc.vector.tensor_tensor(margin[:], scores[m][:].indirect(win_sb[:]), losers[m][:], SUBTRACT)
+            nc.scalar.activation(result[:], margin[:], TANH)
+            nc.sync.dma_start(out=out[P * m : P * (m + 1), :], in_=result[:])

@@ -38,70 +38,79 @@ def tile_picked_ranknet_tanh_e_kernel(tc, xT, w1_words, w1_scales, offs, win, lo
         lose_sb = keep.tile([P, V // PER_COLUMN], U16, name="lose_sb")
         w_codes = keep.tile([P, PASSES, 2 * N], U8, name="w_codes", align_bytes=64)
         w_scales = keep.tile([P, PASSES, N], U8, name="w_scales", align_bytes=64)
-        warm = keep.tile([P, 8], F32, name="warm")
-        warm2 = keep.tile([P, 8], F32, name="warm2")
 
-        rows = xT.rearrange("(g p t) c -> g t p c", p=P, t=PACK)
-        planes = [[keep.tile([P, T], F32, name="plane_%d_%d" % (g, t)) for t in range(PACK)] for g in range(PASSES)]
-        for g in range(PASSES):
-            for t in range(PACK):
-                nc.sync.dma_start(out=planes[g][t][:], in_=rows[g, t])
-                if g == 0 and t == 0:
-                    nc.sync.dma_start(offs_sb[:], offs)
+        rows = xT.rearrange("(g p t) c -> g p t c", p=P, t=PACK)
+        pairs = [keep.tile([P, 2, T], F32, name="pair_%d" % u) for u in range(2)]
+        planes = [keep.tile([P, T], F32, name="plane_%d" % t) for t in range(PACK)]
+        for u in range(2):
+            nc.sync.dma_start(out=pairs[u][:], in_=rows[0, :, 2 * u : 2 * u + 2, :])
+            if u == 0:
+                nc.sync.dma_start(offs_sb[:], offs)
+        for t in range(PACK):
+            nc.sync.dma_start(out=planes[t][:], in_=rows[1, :, t, :])
         nc.sync.dma_start(out=w_codes[:].bitcast(I32), in_=w1_words.rearrange("g p b -> p g b").bitcast(I32))
         nc.sync.dma_start(lose_sb[:], lose)
         nc.sync.dma_start(win_sb[:], win)
 
-        nc.vector.memset(warm[:], 0.0)
-        nc.scalar.activation(warm2[:], warm[:], TANH)
-
-        nc.gpsimd.memset(w_scales[:].rearrange("p g c -> p (g c)").bitcast(I32), 0)
+        nc.vector.memset(w_scales[:].rearrange("p g c -> p (g c)").bitcast(I32), 0)
         for q in range(4):
-            nc.gpsimd.dma_start(
+            nc.scalar.dma_start(
                 out=w_scales[32 * q : 32 * q + 4, :, :].bitcast(I32),
                 in_=w1_scales[:, 4 * q : 4 * q + 4, :].rearrange("g r c -> r g c").bitcast(I32),
             )
 
-        banks = [[psum.tile([P, SLICE], F32, name="bank_%d_%d" % (m, s)) for s in range(SLICES)] for m in range(M_TILES)]
+        widths = (SLICE, S)
+        banks = [[psum.tile([P, w], F32, name="bank_%d_%d" % (m, c)) for c in range(0, S, w)] for m, w in enumerate(widths)]
         scores = [keep.tile([P, S], F32, name="scores_%d" % m) for m in range(M_TILES)]
 
         for g in range(PASSES):
             grouped = [keep.tile([P, HALF, PACK], BF16, name="grouped_%d_%d" % (g, h), align_bytes=64) for h in range(2)]
-            for t in range(PACK):
+            if g == 0:
+                picked = keep.tile([P, PACK, S], F32, name="picked")
+                for t in range(PACK):
+                    nc.vector.tensor_copy(picked[:, t, :], pairs[t // 2][:, t % 2, :].indirect(offs_sb[:]))
                 for h in range(2):
-                    cols = slice(h * HALF // PER_COLUMN, (h + 1) * HALF // PER_COLUMN)
-                    nc.vector.tensor_copy(grouped[h][:, :, t], planes[g][t][:].indirect(offs_sb[:, cols]))
-            x_codes = [keep.tile([P, SLICE], U32, name="x_codes_%d_%d" % (g, s), align_bytes=64) for s in range(SLICES)]
-            x_scales = [keep.tile([P, SLICE], U8, name="x_scales_%d_%d" % (g, s), align_bytes=64) for s in range(SLICES)]
+                    nc.scalar.copy(grouped[h][:], picked[:, :, h * HALF : (h + 1) * HALF].rearrange("p t c -> p c t"))
+            else:
+                for t in range(PACK):
+                    for h in range(2):
+                        cols = slice(h * HALF // PER_COLUMN, (h + 1) * HALF // PER_COLUMN)
+                        nc.vector.tensor_copy(grouped[h][:, :, t], planes[t][:].indirect(offs_sb[:, cols]))
+            x_codes = keep.tile([P, S], U32, name="x_codes_%d" % g, align_bytes=64)
+            x_scales = keep.tile([P, S], U8, name="x_scales_%d" % g, align_bytes=64)
             for s in range(SLICES):
                 h, part = divmod(s, 2)
                 nc.vector.quantize_mx(
-                    out=x_codes[s][:].bitcast(FP8X4),
-                    scales=x_scales[s][:],
+                    out=x_codes[:, s * SLICE : (s + 1) * SLICE].bitcast(FP8X4),
+                    scales=x_scales[:, s * SLICE : (s + 1) * SLICE],
                     in_=grouped[h][:].rearrange("p c t -> p (c t)")[:, part * SLICE * PACK : (part + 1) * SLICE * PACK],
                 )
-            for m in range(M_TILES):
-                for s in range(SLICES):
+            for m, w in enumerate(widths):
+                for c in range(0, S, w):
                     nc.tensor.matmul_mx(
-                        out=banks[m][s][:],
+                        out=banks[m][c // w][:],
                         lhsT=w_codes[:, g, 2 * P * m : 2 * P * (m + 1)].bitcast(FP4X4),
                         lhsT_scale=w_scales[:, g, P * m : P * (m + 1)],
-                        rhs=x_codes[s][:].bitcast(FP8X4),
-                        rhs_scale=x_scales[s][:],
+                        rhs=x_codes[:, c : c + w].bitcast(FP8X4),
+                        rhs_scale=x_scales[:, c : c + w],
                         start=(g == 0),
                         stop=(g == PASSES - 1),
                     )
 
-        for m in range(M_TILES):
-            for s in range(SLICES):
-                nc.scalar.copy(scores[m][:, s * SLICE : (s + 1) * SLICE], banks[m][s][:])
+        for m, w in enumerate(widths):
+            for c in range(0, S, w):
+                nc.scalar.copy(scores[m][:, c : c + w], banks[m][c // w][:])
 
-        losers = [keep.tile([P, V], F32, name="losers_%d" % m) for m in range(M_TILES)]
         for m in range(M_TILES):
-            nc.vector.tensor_copy(losers[m][:], scores[m][:].indirect(lose_sb[:]))
-        for m in range(M_TILES):
+            parts = [slice(lo, lo + V // 2) for lo in range(0, V, V // 2)]
+            lists = [slice(part.start // PER_COLUMN, part.stop // PER_COLUMN) for part in parts]
+            losers = [keep.tile([P, V // 2], F32, name="losers_%d_%d" % (m, i)) for i in range(2)]
             margin = keep.tile([P, V], F32, name="margin_%d" % m)
             result = keep.tile([P, V], F32, name="result_%d" % m)
-            nc.vector.tensor_tensor(margin[:], scores[m][:].indirect(win_sb[:]), losers[m][:], SUBTRACT)
-            nc.scalar.activation(result[:], margin[:], TANH)
-            nc.sync.dma_start(out=out[P * m : P * (m + 1), :], in_=result[:])
+            for i in range(2):
+                nc.vector.tensor_copy(losers[i][:], scores[m][:].indirect(lose_sb[:, lists[i]]))
+            for i in range(2):
+                nc.vector.tensor_tensor(margin[:, parts[i]], scores[m][:].indirect(win_sb[:, lists[i]]), losers[i][:], SUBTRACT)
+            for part in ([slice(0, V)] if m == 0 else parts):
+                nc.scalar.activation(result[:, part], margin[:, part], TANH)
+                nc.sync.dma_start(out=out[P * m : P * (m + 1), part], in_=result[:, part])

@@ -39,15 +39,13 @@ def tile_picked_ranknet_tanh_e_kernel(tc, xT, w1_words, w1_scales, offs, win, lo
         w_codes = keep.tile([P, PASSES, 2 * N], U8, name="w_codes", align_bytes=64)
         w_scales = keep.tile([P, PASSES, N], U8, name="w_scales", align_bytes=64)
 
-        rows = xT.rearrange("(g p t) c -> g p t c", p=P, t=PACK)
-        pairs = [keep.tile([P, 2, T], F32, name="pair_%d" % u) for u in range(2)]
-        planes = [keep.tile([P, T], F32, name="plane_%d" % t) for t in range(PACK)]
-        for u in range(2):
-            nc.sync.dma_start(out=pairs[u][:], in_=rows[0, :, 2 * u : 2 * u + 2, :])
-            if u == 0:
-                nc.sync.dma_start(offs_sb[:], offs)
-        for t in range(PACK):
-            nc.sync.dma_start(out=planes[t][:], in_=rows[1, :, t, :])
+        rows = xT.rearrange("(g p t) c -> g t p c", p=P, t=PACK)
+        planes = [[keep.tile([P, T], F32, name="plane_%d_%d" % (g, t)) for t in range(PACK)] for g in range(PASSES)]
+        for g in range(PASSES):
+            for t in range(PACK):
+                nc.sync.dma_start(out=planes[g][t][:], in_=rows[g, t])
+                if g == 0 and t == 0:
+                    nc.sync.dma_start(offs_sb[:], offs)
         nc.sync.dma_start(out=w_codes[:].bitcast(I32), in_=w1_words.rearrange("g p b -> p g b").bitcast(I32))
         nc.sync.dma_start(lose_sb[:], lose)
         nc.sync.dma_start(win_sb[:], win)
@@ -65,17 +63,10 @@ def tile_picked_ranknet_tanh_e_kernel(tc, xT, w1_words, w1_scales, offs, win, lo
 
         for g in range(PASSES):
             grouped = [keep.tile([P, HALF, PACK], BF16, name="grouped_%d_%d" % (g, h), align_bytes=64) for h in range(2)]
-            if g == 0:
-                picked = keep.tile([P, PACK, S], F32, name="picked")
-                for t in range(PACK):
-                    nc.vector.tensor_copy(picked[:, t, :], pairs[t // 2][:, t % 2, :].indirect(offs_sb[:]))
+            for t in range(PACK):
                 for h in range(2):
-                    nc.scalar.copy(grouped[h][:], picked[:, :, h * HALF : (h + 1) * HALF].rearrange("p t c -> p c t"))
-            else:
-                for t in range(PACK):
-                    for h in range(2):
-                        cols = slice(h * HALF // PER_COLUMN, (h + 1) * HALF // PER_COLUMN)
-                        nc.vector.tensor_copy(grouped[h][:, :, t], planes[t][:].indirect(offs_sb[:, cols]))
+                    cols = slice(h * HALF // PER_COLUMN, (h + 1) * HALF // PER_COLUMN)
+                    nc.vector.tensor_copy(grouped[h][:, :, t], planes[g][t][:].indirect(offs_sb[:, cols]))
             x_codes = keep.tile([P, S], U32, name="x_codes_%d" % g, align_bytes=64)
             x_scales = keep.tile([P, S], U8, name="x_scales_%d" % g, align_bytes=64)
             for s in range(SLICES):

from contextlib import ExitStack

import concourse.mybir as mybir

K, T, S, V, N = 1024, 2048, 512, 256, 256
FLOPS = 2 * K * N * S

F32 = mybir.dt.float32
BF16 = mybir.dt.bfloat16
I32 = mybir.dt.int32
U32 = mybir.dt.uint32
U16 = mybir.dt.uint16
U8 = mybir.dt.uint8
FP8X4 = mybir.dt.float8_e4m3fn_x4
FP4X4 = mybir.dt.float4_e2m1fn_x4
TANH = mybir.ActivationFunctionType.Tanh
SUBTRACT = mybir.AluOpType.subtract

P = 128
PACK = 4
K_PASS = P * PACK
PASSES = K // K_PASS
M_TILES = N // P
HALF = S // 2
SLICE = 128
SLICES = S // SLICE
PER_COLUMN = 16


def tile_picked_ranknet_tanh_e_kernel(tc, xT, w1_words, w1_scales, offs, win, lose, out):
    nc = tc.nc
    with ExitStack() as ctx:
        keep = ctx.enter_context(tc.tile_pool(name="keep", bufs=1))
        psum = ctx.enter_context(tc.psum_pool(name="psum", bufs=1))

        offs_sb = keep.tile([P, S // PER_COLUMN], U16, name="offs_sb")
        win_sb = keep.tile([P, V // PER_COLUMN], U16, name="win_sb")
        lose_sb = keep.tile([P, V // PER_COLUMN], U16, name="lose_sb")
        w_codes = keep.tile([P, PASSES, 2 * N], U8, name="w_codes", align_bytes=64)
        w_scales = keep.tile([P, PASSES, N], U8, name="w_scales", align_bytes=64)

        rows = xT.rearrange("(g p t) c -> g t p c", p=P, t=PACK)
        planes = [[keep.tile([P, T], F32, name="plane_%d_%d" % (g, t)) for t in range(PACK)] for g in range(PASSES)]
        for g in range(PASSES):
            for t in range(PACK):
                nc.sync.dma_start(out=planes[g][t][:], in_=rows[g, t])
                if g == 0 and t == 0:
                    nc.sync.dma_start(offs_sb[:], offs)
        nc.sync.dma_start(out=w_codes[:].bitcast(I32), in_=w1_words.rearrange("g p b -> p g b").bitcast(I32))
        nc.sync.dma_start(lose_sb[:], lose)
        nc.sync.dma_start(win_sb[:], win)

        nc.vector.memset(w_scales[:].rearrange("p g c -> p (g c)").bitcast(I32), 0)
        for q in range(4):
            nc.scalar.dma_start(
                out=w_scales[32 * q : 32 * q + 4, :, :].bitcast(I32),
                in_=w1_scales[:, 4 * q : 4 * q + 4, :].rearrange("g r c -> r g c").bitcast(I32),
            )

        widths = (SLICE, S)
        banks = [[psum.tile([P, w], F32, name="bank_%d_%d" % (m, c)) for c in range(0, S, w)] for m, w in enumerate(widths)]
        scores = [keep.tile([P, S], F32, name="scores_%d" % m) for m in range(M_TILES)]

        for g in range(PASSES):
            grouped = [keep.tile([P, HALF, PACK], BF16, name="grouped_%d_%d" % (g, h), align_bytes=64) for h in range(2)]
            for t in range(PACK):
                for h in range(2):
                    cols = slice(h * HALF // PER_COLUMN, (h + 1) * HALF // PER_COLUMN)
                    nc.vector.tensor_copy(grouped[h][:, :, t], planes[g][t][:].indirect(offs_sb[:, cols]))
            x_codes = keep.tile([P, S], U32, name="x_codes_%d" % g, align_bytes=64)
            x_scales = keep.tile([P, S], U8, name="x_scales_%d" % g, align_bytes=64)
            for s in range(SLICES):
                h, part = divmod(s, 2)
                nc.vector.quantize_mx(
                    out=x_codes[:, s * SLICE : (s + 1) * SLICE].bitcast(FP8X4),
                    scales=x_scales[:, s * SLICE : (s + 1) * SLICE],
                    in_=grouped[h][:].rearrange("p c t -> p (c t)")[:, part * SLICE * PACK : (part + 1) * SLICE * PACK],
                )
            for m, w in enumerate(widths):
                for c in range(0, S, w):
                    nc.tensor.matmul_mx(
                        out=banks[m][c // w][:],
                        lhsT=w_codes[:, g, 2 * P * m : 2 * P * (m + 1)].bitcast(FP4X4),
                        lhsT_scale=w_scales[:, g, P * m : P * (m + 1)],
                        rhs=x_codes[:, c : c + w].bitcast(FP8X4),
                        rhs_scale=x_scales[:, c : c + w],
                        start=(g == 0),
                        stop=(g == PASSES - 1),
                    )

        for m, w in enumerate(widths):
            for c in range(0, S, w):
                nc.scalar.copy(scores[m][:, c : c + w], banks[m][c // w][:])

        for m in range(M_TILES):
            parts = [slice(lo, lo + V // 2) for lo in range(0, V, V // 2)]
            lists = [slice(part.start // PER_COLUMN, part.stop // PER_COLUMN) for part in parts]
            losers = [keep.tile([P, V // 2], F32, name="losers_%d_%d" % (m, i)) for i in range(2)]
            margin = keep.tile([P, V], F32, name="margin_%d" % m)
            result = keep.tile([P, V], F32, name="result_%d" % m)
            for i in range(2):
                nc.vector.tensor_copy(losers[i][:], scores[m][:].indirect(lose_sb[:, lists[i]]))
            for i in range(2):
                nc.vector.tensor_tensor(margin[:, parts[i]], scores[m][:].indirect(win_sb[:, lists[i]]), losers[i][:], SUBTRACT)
            for part in ([slice(0, V)] if m == 0 else parts):
                nc.scalar.activation(result[:, part], margin[:, part], TANH)
                nc.sync.dma_start(out=out[P * m : P * (m + 1), part], in_=result[:, part])
